import numpy as np
import ml_dtypes


def mxq(x, axis, fmt="e4m3"):
    dtype, down = {"e4m3": (ml_dtypes.float8_e4m3fn, 7), "e5m2": (ml_dtypes.float8_e5m2, 14)}[fmt]
    v = np.moveaxis(np.asarray(x, np.float32).astype(ml_dtypes.bfloat16).astype(np.float64), axis, -1)
    blocks = v.reshape(v.shape[:-1] + (-1, 32))
    amax = np.abs(blocks).max(-1, keepdims=True)
    byte = np.maximum(np.where(amax > 0, np.frexp(amax)[1] - 1 + 127, 0) - down, 1)
    scale = np.exp2(byte - 127.0)
    codes = (blocks / scale).astype(np.float32).astype(dtype).astype(np.float64)
    return np.moveaxis((codes * scale).reshape(v.shape), -1, axis)


WIDE = False


def mx_kscale(k):
    if not WIDE:
        return np.ones(k)
    levels = np.array([30, -30])
    if k % 512:
        return np.exp2(np.random.permutation(np.resize(levels, k // 32))).repeat(32)
    a = np.empty((k // 512, 16))
    for p in range(k // 512):
        a[p, :8] = np.random.permutation(np.resize(levels, 8))
        for g in range(8):
            far = levels[np.abs(levels - a[p, g]) >= 10]
            a[p, g + 8] = far[np.random.randint(len(far))]
    return np.exp2(a.ravel()).repeat(32)


def f64(x):
    return np.asarray(x).astype(np.float64)


def striped(idx):
    return np.tile(np.asarray(idx).reshape(-1, 16).T, (8, 1)).astype(np.uint16)


def unstriped(offs):
    return offs[:16].T.reshape(-1).astype(np.int64)


def striped8(idx):
    return np.asarray(idx).reshape(8, -1, 16).transpose(0, 2, 1).reshape(128, -1).astype(np.uint16)


def unstriped8(offs):
    return offs.reshape(8, 16, -1).transpose(0, 2, 1).reshape(8, -1).astype(np.int64)


def pick8(x, idx, run):
    r = np.arange(len(x))
    return x[r[:, None], idx[r % (8 * run) // run]]


E2M1 = np.array([0.0, 0.5, 1.0, 1.5, 2.0, 3.0, 4.0, 6.0, -0.0, -0.5, -1.0, -1.5, -2.0, -3.0, -4.0, -6.0])


def pack_weight(w, fmt):
    k, n = w.shape
    w = f64(np.asarray(w, np.float32).astype(ml_dtypes.bfloat16)).reshape(k // 32, 32, n)
    amax = np.abs(w).max(1)
    if fmt == "e4m3":
        byte = np.frexp(amax)[1] - 1 + 127 - 7
    else:
        mant, ex = np.frexp(amax / 6.0)
        byte = np.where(mant > 0.5, ex, ex - 1) + 127
    byte = np.clip(np.where(amax > 0, byte, 1), 1, 254)
    scaled = (w * np.exp2(127.0 - byte)[:, None, :]).reshape(k, n).astype(np.float32)
    by_word = np.ascontiguousarray(scaled.reshape(k // 512, 128, 4, n).transpose(0, 1, 3, 2))
    if fmt == "e4m3":
        words = by_word.astype(ml_dtypes.float8_e4m3fn).view(np.uint8)
    else:
        c = by_word.astype(ml_dtypes.float4_e2m1fn).view(np.uint8) & 0xF
        words = (c[..., 0::2] | (c[..., 1::2] << 4)).reshape(k // 512, 128, 2 * n)
    return np.ascontiguousarray(words), np.ascontiguousarray(byte.astype(np.uint8).reshape(k // 512, 16, n))


def unpack_weight(words, scales, fmt):
    g, _, n = scales.shape
    words = np.ascontiguousarray(words).reshape(g, 128, n, -1)
    if fmt == "e4m3":
        vals = words.view(ml_dtypes.float8_e4m3fn).astype(np.float64)
    else:
        nib = np.empty((g, 128, n, 4), np.uint8)
        nib[..., 0::2] = words & 0xF
        nib[..., 1::2] = words >> 4
        vals = E2M1[nib]
    vals = vals * np.repeat(np.exp2(scales.astype(np.float64) - 127.0), 8, axis=1)[..., None]
    return vals.transpose(0, 1, 3, 2).reshape(g * 512, n)


K, J, N, R, T, V = 512, 512, 256, 256, 1024, 1024


def setup_inputs():
    n = np.random.standard_normal
    idx = np.stack([np.random.permutation(T)[:J] for _ in range(8)])
    idx2 = np.random.permutation(V)[:J]
    fj = mx_kscale(J)
    fk = mx_kscale(K)
    drp = pack_weight(n((K, R)) * 1 / np.sqrt(K) / fk[:, None], "e4m3")
    return {
        "xf": (n((K, T))).astype(np.float32),
        "ra": (np.random.uniform(0.5, 1.5, (1, J)) * fj).astype(np.float32),
        "gt": (n((N, V)) * np.exp(0.5 * n((1, V)))).astype(np.float32),
        "cb": (np.random.uniform(0.5, 1.5, (J, 1)) / fj[:, None]).astype(np.float32),
        "fkr": (np.random.uniform(0.5, 1.5, (1, K)) * fk).astype(np.float32),
        "dr_words": drp[0],
        "dr_scales": drp[1],
        "bn": (np.random.uniform(-12.0, 12.0, (1, N))).astype(np.float32),
        "offs": striped8(idx),
        "offs2": striped(idx2),
    }


def reference(xf, ra, gt, cb, fkr, dr_words, dr_scales, bn, offs, offs2):
    idx = unstriped8(offs)
    idx2 = unstriped(offs2)
    dru = unpack_weight(dr_words, dr_scales, "e4m3")
    us = pick8(f64(xf), idx, 64) * f64(ra)
    ut = us.T
    uj = ut * f64(fkr)
    gr1 = f64(gt)[:, idx2].T
    gj = gr1 / (np.max(np.abs(gr1), axis=1, keepdims=True) + 0.2) * f64(cb)
    ujq = mxq(uj, 0, "e4m3")
    gjq = mxq(gj, 0, "e5m2")
    w = ujq.T @ gjq
    wq = mxq(w, 0, "e5m2")
    v2 = dru.T @ wq
    wv = v2 + f64(bn)
    mn = np.mean(wv, axis=1, keepdims=True)
    dw = wv - mn
    y = dw / (np.mean(np.abs(dw), axis=1, keepdims=True) + 2.0)
    return y

@@ -1,0 +1,255 @@
+from contextlib import ExitStack
+
+import concourse.mybir as mybir
+from concourse.masks import make_identity
+
+K, J, N, R, T, V = 512, 512, 256, 256, 1024, 1024
+FLOPS = 2 * K * J * N + 2 * R * K * N
+
+F32 = mybir.dt.float32
+BF16 = mybir.dt.bfloat16
+U32 = mybir.dt.uint32
+I32 = mybir.dt.int32
+U16 = mybir.dt.uint16
+U8 = mybir.dt.uint8
+E4M3 = mybir.dt.float8_e4m3fn_x4
+E5M2 = mybir.dt.float8_e5m2_x4
+ALU = mybir.AluOpType
+ACT = mybir.ActivationFunctionType
+P = 128
+PACK = 4
+
+
+def tile_list_directions_headpicks_sized_spread_kernel(
+    tc, xf, ra, gt, cb, fkr, dr_words, dr_scales, bn, offs, offs2, out
+):
+    nc = tc.nc
+    with ExitStack() as ctx:
+        keep = ctx.enter_context(tc.tile_pool(name="keep", bufs=1))
+        psum = ctx.enter_context(tc.psum_pool(name="psum", bufs=1))
+
+        lists = keep.tile([P, J // 16], U16, name="lists")
+        list2 = keep.tile([P, J // 16], U16, name="list2")
+        g_tab = [keep.tile([P, V], F32, name="g_tab%d" % m) for m in range(2)]
+        x_tab = [keep.tile([P, T], F32, name="x_tab%d" % i) for i in range(PACK)]
+        ra_c = keep.tile([P, PACK], F32, name="ra_c")
+        cb_c = keep.tile([P, PACK], F32, name="cb_c")
+        fk_c = keep.tile([P, PACK], F32, name="fk_c")
+        dr_codes = keep.tile([P, R], U32, name="dr_codes", align_bytes=64)
+        dr_plane = keep.tile([P, R], U8, name="dr_plane", align_bytes=64)
+        bn_b = keep.tile([P, N], F32, name="bn_b")
+        ident = keep.tile([P, P], F32, name="ident")
+
+        x_rows = xf.rearrange("(p i) t -> p i t", i=PACK)
+        nc.sync.dma_start(g_tab[0][:], gt[0:P, :])
+        nc.sync.dma_start(list2[:], offs2)
+        nc.sync.dma_start(ra_c[:], ra.rearrange("o (q s) -> (o q) s", s=PACK))
+        nc.sync.dma_start(cb_c[:], cb.rearrange("(q s) o -> q (s o)", s=PACK))
+        nc.sync.dma_start(g_tab[1][:], gt[P : 2 * P, :])
+        nc.sync.dma_start(x_tab[0][:], x_rows[:, 0, :])
+        nc.sync.dma_start(lists[:], offs)
+        nc.sync.dma_start(fk_c[:], fkr.rearrange("o (p i) -> (o p) i", i=PACK))
+        for i in range(1, PACK):
+            nc.sync.dma_start(x_tab[i][:], x_rows[:, i, :])
+        nc.gpsimd.memset(dr_plane[:].bitcast(I32), 0)
+        make_identity(nc, ident[:])
+        nc.sync.dma_start(
+            dr_codes[:].bitcast(I32),
+            dr_words[0].rearrange("p c r -> p (c r)").bitcast(I32),
+        )
+        for q in range(4):
+            nc.sync.dma_start(
+                dr_plane[32 * q : 32 * q + 4, :].bitcast(I32),
+                dr_scales[0, 4 * q : 4 * q + 4, :].bitcast(I32),
+            )
+        nc.sync.dma_start(bn_b[:], bn[0].partition_broadcast(P))
+
+        half = J // 2
+        hc = half // 16
+
+        def gather_split(dst, table, offsets):
+            nc.vector.tensor_copy(dst[:, 0:half], table[:].indirect(offsets[:, 0:hc]))
+            nc.scalar.activation(dst[:, half:J], table[:].indirect(offsets[:, hc : 2 * hc]), ACT.Copy)
+
+        ra_bank = psum.tile([P, PACK, P], F32, name="ra_bank")
+        for s in range(PACK):
+            nc.tensor.transpose(ra_bank[:, s, :], ra_c[:, s : s + 1].to_broadcast([P, P]), ident[:])
+
+        cb_inv = keep.tile([P, PACK], F32, name="cb_inv")
+        nc.vector.reciprocal(cb_inv[:], cb_c[:])
+        g_abs = [keep.tile([P, PACK, P + m], F32, name="g_abs%d" % m) for m in range(2)]
+        g_bank = []
+        for m in range(2):
+            picked = keep.tile([P, J], F32, name="g_picked%d" % m, tag="g_picked0" if m == 0 else "ring1")
+            gather_split(picked, g_tab[m], list2)
+            bank = psum.tile([P, PACK, P], F32, name="g_bank%d" % m, tag="gv%d" % m)
+            for s in range(PACK):
+                nc.tensor.transpose(bank[:, s, :], picked[:, s:J:PACK], ident[:])
+            g_bank.append(bank)
+
+        x_picked = {}
+        u_rounded = [keep.tile([P, J], BF16, name="u_rounded%d" % i) for i in range(PACK)]
+        u_grouped = {
+            first: keep.tile([P, count * J], BF16, name="u_grouped%d" % first, align_bytes=64)
+            for first, count in ((0, 2), (2, 1), (3, 1))
+        }
+        u_codes = keep.tile([P, PACK * P], U32, name="u_codes", align_bytes=64)
+        u_plane = keep.tile([P, PACK * P], U8, name="u_plane", align_bytes=64)
+        u_early = psum.tile([P, 2, 2, P], F32, name="u_early")
+        u_late = [psum.tile([P, 1, 2, P], F32, name="u_late%d" % i) for i in range(2)]
+        u_bank = [u_early[:, 0], u_early[:, 1], u_late[0][:, 0], u_late[1][:, 0]]
+
+        def weigh(i):
+            nc.vector.scalar_tensor_tensor(
+                out=u_rounded[i][:].rearrange("p (q s) -> p q s", s=PACK),
+                in0=x_picked[i][:].rearrange("p (q s) -> p q s", s=PACK),
+                scalar=fk_c[:, i : i + 1],
+                in1=ra_bank[:].rearrange("p s q -> p q s"),
+                op0=ALU.mult,
+                op1=ALU.mult,
+            )
+            words = u_rounded[i][:].bitcast(F32)
+            for u in range(2):
+                nc.tensor.transpose(u_bank[i][:, u, :], words[:, u : J // 2 : 2], ident[:])
+
+        def regroup(bank, first, count):
+            nc.scalar.copy(
+                u_grouped[first][:].bitcast(F32).rearrange("q (i p u) -> q i p u", i=count, u=2),
+                bank[:].rearrange("q i u p -> q i p u"),
+            )
+
+        def quantise_u(first, count):
+            cols = slice(first * P, (first + count) * P)
+            nc.vector.quantize_mx(
+                u_codes[:, cols].bitcast(E4M3),
+                u_plane[:, cols],
+                u_grouped[first][:],
+            )
+
+        def pick_tile(i):
+            x_picked[i] = keep.tile([P, J], F32, name="x_picked%d" % i, tag="ring%d" % (i % 2))
+            return x_picked[i]
+
+        nc.scalar.activation(g_abs[0][:], g_bank[0][:], ACT.Abs)
+        gather_split(pick_tile(0), x_tab[0], lists)
+        nc.scalar.activation(g_abs[1][:, :, 0:P], g_bank[1][:], ACT.Abs)
+        weigh(0)
+        nc.vector.tensor_reduce(g_abs[1][:, :, P], g_abs[0][:], mybir.AxisListType.X, ALU.max)
+        nc.scalar.activation(pick_tile(1)[:], x_tab[1][:].indirect(lists[:]), ACT.Copy)
+        g_max = keep.tile([P, PACK], F32, name="g_max")
+        nc.vector.tensor_reduce(g_max[:], g_abs[1][:], mybir.AxisListType.X, ALU.max)
+        g_den = keep.tile([P, PACK], F32, name="g_den")
+        nc.vector.scalar_tensor_tensor(g_den[:], g_max[:], 0.2, cb_inv[:], ALU.add, ALU.mult)
+        g_fac = keep.tile([P, PACK], F32, name="g_fac")
+        nc.vector.reciprocal(g_fac[:], g_den[:])
+        nc.scalar.activation(pick_tile(2)[:], x_tab[2][:].indirect(lists[:]), ACT.Copy)
+        weigh(1)
+        nc.scalar.activation(pick_tile(3)[:], x_tab[3][:].indirect(lists[:]), ACT.Copy)
+        g_grouped = keep.tile([P, N, PACK], BF16, name="g_grouped", align_bytes=64)
+        for m in range(2):
+            nc.vector.tensor_tensor(
+                g_grouped[:, m * P : (m + 1) * P, :],
+                g_bank[m][:].rearrange("q s n -> q n s"),
+                g_fac[:].unsqueeze(1).to_broadcast([P, P, PACK]),
+                ALU.mult,
+            )
+        weigh(2)
+        weigh(3)
+        regroup(u_early, 0, 2)
+        regroup(u_late[0], 2, 1)
+        regroup(u_late[1], 3, 1)
+        g_codes = keep.tile([P, N], U32, name="g_codes", align_bytes=64)
+        g_plane = keep.tile([P, N], U8, name="g_plane", align_bytes=64)
+        nc.vector.quantize_mx(g_codes[:].bitcast(E5M2), g_plane[:], g_grouped[:].rearrange("q n s -> q (n s)"))
+        quantise_u(0, 2)
+        quantise_u(2, 1)
+        quantise_u(3, 1)
+        w_bank = [psum.tile([P, PACK, P], F32, name="w_bank%d" % h) for h in range(2)]
+
+        def moment(i):
+            for h in range(2):
+                cols = slice(h * P, (h + 1) * P)
+                nc.tensor.matmul_mx(
+                    out=w_bank[h][:, i, :],
+                    lhsT=u_codes[:, i * P : (i + 1) * P].bitcast(E4M3),
+                    lhsT_scale=u_plane[:, i * P : (i + 1) * P],
+                    rhs=g_codes[:, cols].bitcast(E5M2),
+                    rhs_scale=g_plane[:, cols],
+                    start=True,
+                    stop=True,
+                )
+
+        for i in range(PACK):
+            moment(i)
+
+        w_grouped = keep.tile([P, N, PACK], BF16, name="w_grouped", align_bytes=64)
+        w_codes = keep.tile([P, N], U32, name="w_codes", align_bytes=64)
+        w_plane = keep.tile([P, N], U8, name="w_plane", align_bytes=64)
+        nc.vector.tensor_copy(w_grouped[:, 0:P, :], w_bank[0][:].rearrange("p i n -> p n i"))
+        nc.scalar.copy(w_grouped[:, P:N, :], w_bank[1][:].rearrange("p i n -> p n i"))
+        for h in range(2):
+            cols = slice(h * P, (h + 1) * P)
+            nc.vector.quantize_mx(
+                w_codes[:, cols].bitcast(E5M2),
+                w_plane[:, cols],
+                w_grouped[:, cols, :].rearrange("p n i -> p (n i)"),
+            )
+
+        neg = keep.tile([P, 2, N], F32, name="neg")
+        neg_sum = keep.tile([P, 2], F32, name="neg_sum")
+        dev = keep.tile([P, 2, N], F32, name="dev")
+        dev_abs = keep.tile([P, 2, N], F32, name="dev_abs")
+        abs_sum = keep.tile([P, 2], F32, name="abs_sum")
+        root = keep.tile([P, 2], F32, name="root")
+        two_n = keep.tile([P, 1], F32, name="two_n")
+        nc.gpsimd.memset(two_n[:], 2.0 * N)
+        y = [keep.tile([P, N], F32, name="y%d" % t) for t in range(2)]
+        v_bank = []
+        for t in range(2):
+            bank = psum.tile([P, N], F32, name="v_bank%d" % t, tag="gv%d" % t)
+            v_bank.append(bank)
+        for h in range(2):
+            cols = slice(h * P, (h + 1) * P)
+            for t in range(2):
+                rows = slice(t * P, (t + 1) * P)
+                nc.tensor.matmul_mx(
+                    out=v_bank[t][:, cols],
+                    lhsT=dr_codes[:, rows].bitcast(E4M3),
+                    lhsT_scale=dr_plane[:, rows],
+                    rhs=w_codes[:, cols].bitcast(E5M2),
+                    rhs_scale=w_plane[:, cols],
+                    start=True,
+                    stop=True,
+                )
+        for t in range(2):
+            nc.vector.scalar_tensor_tensor(
+                out=neg[:, t, :],
+                in0=v_bank[t][:],
+                scalar=-1.0,
+                in1=bn_b[:],
+                op0=ALU.mult,
+                op1=ALU.subtract,
+                accum_out=neg_sum[:, t : t + 1],
+            )
+            nc.scalar.activation(
+                dev_abs[:, t, :],
+                neg[:, t, :],
+                ACT.Abs,
+                bias=neg_sum[:, t : t + 1],
+                scale=-float(N),
+                accum_out=abs_sum[:, t : t + 1],
+            )
+        for t in range(2):
+            nc.vector.tensor_scalar(
+                dev[:, t, :], neg[:, t, :], -float(N), neg_sum[:, t : t + 1], ALU.mult, ALU.add
+            )
+        for t in range(2):
+            nc.scalar.activation(
+                root[:, t : t + 1], abs_sum[:, t : t + 1], ACT.Abs_reciprocal_sqrt, bias=two_n[:], scale=1.0 / N
+            )
+        for t in range(2):
+            nc.vector.tensor_scalar(
+                y[t][:], dev[:, t, :], root[:, t : t + 1], root[:, t : t + 1], ALU.mult, ALU.mult
+            )
+        nc.sync.dma_start(out[0:P, :], y[0][:])
+        nc.scalar.dma_start(out[P : 2 * P, :], y[1][:])

@@ -51,6 +51,9 @@ def tile_list_directions_headpicks_sized_spread_kernel(
         nc.sync.dma_start(fk_c[:], fkr.rearrange("o (p i) -> (o p) i", i=PACK))
         for i in range(1, PACK):
             nc.sync.dma_start(x_tab[i][:], x_rows[:, i, :])
+        warm = keep.tile([P, 2], F32, name="warm")
+        nc.vector.memset(warm[:, 0:1], 1.0)
+        nc.scalar.activation(warm[:, 1:2], warm[:, 0:1], ACT.Abs_reciprocal_sqrt)
         nc.gpsimd.memset(dr_plane[:].bitcast(I32), 0)
         make_identity(nc, ident[:])
         nc.sync.dma_start(

@@ -43,11 +43,11 @@ def tile_list_directions_headpicks_sized_spread_kernel(
         x_rows = xf.rearrange("(p i) t -> p i t", i=PACK)
         nc.sync.dma_start(g_tab[0][:], gt[0:P, :])
         nc.sync.dma_start(list2[:], offs2)
-        nc.sync.dma_start(ra_c[:], ra.rearrange("o (q s) -> (o q) s", s=PACK))
-        nc.sync.dma_start(cb_c[:], cb.rearrange("(q s) o -> q (s o)", s=PACK))
         nc.sync.dma_start(g_tab[1][:], gt[P : 2 * P, :])
         nc.sync.dma_start(x_tab[0][:], x_rows[:, 0, :])
         nc.sync.dma_start(lists[:], offs)
+        nc.sync.dma_start(cb_c[:], cb.rearrange("(q s) o -> q (s o)", s=PACK))
+        nc.sync.dma_start(ra_c[:], ra.rearrange("o (q s) -> (o q) s", s=PACK))
         nc.sync.dma_start(fk_c[:], fkr.rearrange("o (p i) -> (o p) i", i=PACK))
         for i in range(1, PACK):
             nc.sync.dma_start(x_tab[i][:], x_rows[:, i, :])
@@ -74,13 +74,7 @@ def tile_list_directions_headpicks_sized_spread_kernel(
             nc.vector.tensor_copy(dst[:, 0:half], table[:].indirect(offsets[:, 0:hc]))
             nc.scalar.activation(dst[:, half:J], table[:].indirect(offsets[:, hc : 2 * hc]), ACT.Copy)
 
-        ra_bank = psum.tile([P, PACK, P], F32, name="ra_bank")
-        for s in range(PACK):
-            nc.tensor.transpose(ra_bank[:, s, :], ra_c[:, s : s + 1].to_broadcast([P, P]), ident[:])
-
-        cb_inv = keep.tile([P, PACK], F32, name="cb_inv")
-        nc.vector.reciprocal(cb_inv[:], cb_c[:])
-        g_abs = [keep.tile([P, PACK, P + m], F32, name="g_abs%d" % m) for m in range(2)]
+        g_abs = [keep.tile([P, PACK, P + 4 * m], F32, name="g_abs%d" % m, tag="g_abs%d" % m) for m in range(2)]
         g_bank = []
         for m in range(2):
             picked = keep.tile([P, J], F32, name="g_picked%d" % m, tag="g_picked0" if m == 0 else "ring1")
@@ -90,8 +84,13 @@ def tile_list_directions_headpicks_sized_spread_kernel(
                 nc.tensor.transpose(bank[:, s, :], picked[:, s:J:PACK], ident[:])
             g_bank.append(bank)
 
+        ra_bank = psum.tile([P, PACK, P], F32, name="ra_bank")
+        for s in range(PACK):
+            nc.tensor.transpose(ra_bank[:, s, :], ra_c[:, s : s + 1].to_broadcast([P, P]), ident[:])
+
+        cb_inv = keep.tile([P, PACK], F32, name="cb_inv")
+        nc.vector.reciprocal(cb_inv[:], cb_c[:])
         x_picked = {}
-        u_rounded = [keep.tile([P, J], BF16, name="u_rounded%d" % i) for i in range(PACK)]
         u_grouped = {
             first: keep.tile([P, count * J], BF16, name="u_grouped%d" % first, align_bytes=64)
             for first, count in ((0, 2), (2, 1), (3, 1))
@@ -103,15 +102,16 @@ def tile_list_directions_headpicks_sized_spread_kernel(
         u_bank = [u_early[:, 0], u_early[:, 1], u_late[0][:, 0], u_late[1][:, 0]]
 
         def weigh(i):
+            rounded = keep.tile([P, J], BF16, name="u_rounded%d" % i, tag=("x_tab1", "g_abs1", "g_max", "round3")[i])
             nc.vector.scalar_tensor_tensor(
-                out=u_rounded[i][:].rearrange("p (q s) -> p q s", s=PACK),
+                out=rounded[:].rearrange("p (q s) -> p q s", s=PACK),
                 in0=x_picked[i][:].rearrange("p (q s) -> p q s", s=PACK),
                 scalar=fk_c[:, i : i + 1],
                 in1=ra_bank[:].rearrange("p s q -> p q s"),
                 op0=ALU.mult,
                 op1=ALU.mult,
             )
-            words = u_rounded[i][:].bitcast(F32)
+            words = rounded[:].bitcast(F32)
             for u in range(2):
                 nc.tensor.transpose(u_bank[i][:, u, :], words[:, u : J // 2 : 2], ident[:])
 
@@ -130,41 +130,51 @@ def tile_list_directions_headpicks_sized_spread_kernel(
             )
 
         def pick_tile(i):
-            x_picked[i] = keep.tile([P, J], F32, name="x_picked%d" % i, tag="ring%d" % (i % 2))
+            x_picked[i] = keep.tile([P, J], F32, name="x_picked%d" % i, tag="ring%d" % i)
             return x_picked[i]
 
         nc.scalar.activation(g_abs[0][:], g_bank[0][:], ACT.Abs)
         gather_split(pick_tile(0), x_tab[0], lists)
         nc.scalar.activation(g_abs[1][:, :, 0:P], g_bank[1][:], ACT.Abs)
-        weigh(0)
         nc.vector.tensor_reduce(g_abs[1][:, :, P], g_abs[0][:], mybir.AxisListType.X, ALU.max)
-        nc.scalar.activation(pick_tile(1)[:], x_tab[1][:].indirect(lists[:]), ACT.Copy)
+        gather_split(pick_tile(1), x_tab[1], lists)
         g_max = keep.tile([P, PACK], F32, name="g_max")
-        nc.vector.tensor_reduce(g_max[:], g_abs[1][:], mybir.AxisListType.X, ALU.max)
+        nc.vector.tensor_reduce(g_max[:], g_abs[1][:, :, 0 : P + 1], mybir.AxisListType.X, ALU.max)
         g_den = keep.tile([P, PACK], F32, name="g_den")
         nc.vector.scalar_tensor_tensor(g_den[:], g_max[:], 0.2, cb_inv[:], ALU.add, ALU.mult)
         g_fac = keep.tile([P, PACK], F32, name="g_fac")
         nc.vector.reciprocal(g_fac[:], g_den[:])
-        nc.scalar.activation(pick_tile(2)[:], x_tab[2][:].indirect(lists[:]), ACT.Copy)
+        weigh(0)
         weigh(1)
+        nc.scalar.activation(pick_tile(2)[:], x_tab[2][:].indirect(lists[:]), ACT.Copy)
+        weigh(2)
         nc.scalar.activation(pick_tile(3)[:], x_tab[3][:].indirect(lists[:]), ACT.Copy)
         g_grouped = keep.tile([P, N, PACK], BF16, name="g_grouped", align_bytes=64)
-        for m in range(2):
+
+        def scale_g(m):
             nc.vector.tensor_tensor(
                 g_grouped[:, m * P : (m + 1) * P, :],
                 g_bank[m][:].rearrange("q s n -> q n s"),
                 g_fac[:].unsqueeze(1).to_broadcast([P, P, PACK]),
                 ALU.mult,
             )
-        weigh(2)
+
+        scale_g(0)
         weigh(3)
+        scale_g(1)
         regroup(u_early, 0, 2)
         regroup(u_late[0], 2, 1)
         regroup(u_late[1], 3, 1)
         g_codes = keep.tile([P, N], U32, name="g_codes", align_bytes=64)
         g_plane = keep.tile([P, N], U8, name="g_plane", align_bytes=64)
-        nc.vector.quantize_mx(g_codes[:].bitcast(E5M2), g_plane[:], g_grouped[:].rearrange("q n s -> q (n s)"))
         quantise_u(0, 2)
+        for h in range(2):
+            cols = slice(h * P, (h + 1) * P)
+            nc.vector.quantize_mx(
+                g_codes[:, cols].bitcast(E5M2),
+                g_plane[:, cols],
+                g_grouped[:, cols, :].rearrange("q n s -> q (n s)"),
+            )
         quantise_u(2, 1)
         quantise_u(3, 1)
         w_bank = [psum.tile([P, PACK, P], F32, name="w_bank%d" % h) for h in range(2)]

from contextlib import ExitStack

import concourse.mybir as mybir
from concourse.masks import make_identity

K, J, N, R, T, V = 512, 512, 256, 256, 1024, 1024
FLOPS = 2 * K * J * N + 2 * R * K * N

F32 = mybir.dt.float32
BF16 = mybir.dt.bfloat16
U32 = mybir.dt.uint32
I32 = mybir.dt.int32
U16 = mybir.dt.uint16
U8 = mybir.dt.uint8
E4M3 = mybir.dt.float8_e4m3fn_x4
E5M2 = mybir.dt.float8_e5m2_x4
ALU = mybir.AluOpType
ACT = mybir.ActivationFunctionType
P = 128
PACK = 4


def tile_list_directions_headpicks_sized_spread_kernel(
    tc, xf, ra, gt, cb, fkr, dr_words, dr_scales, bn, offs, offs2, out
):
    nc = tc.nc
    with ExitStack() as ctx:
        keep = ctx.enter_context(tc.tile_pool(name="keep", bufs=1))
        psum = ctx.enter_context(tc.psum_pool(name="psum", bufs=1))

        lists = keep.tile([P, J // 16], U16, name="lists")
        list2 = keep.tile([P, J // 16], U16, name="list2")
        g_tab = [keep.tile([P, V], F32, name="g_tab%d" % m) for m in range(2)]
        x_tab = [keep.tile([P, T], F32, name="x_tab%d" % i) for i in range(PACK)]
        ra_c = keep.tile([P, PACK], F32, name="ra_c")
        cb_c = keep.tile([P, PACK], F32, name="cb_c")
        fk_c = keep.tile([P, PACK], F32, name="fk_c")
        dr_codes = keep.tile([P, R], U32, name="dr_codes", align_bytes=64)
        dr_plane = keep.tile([P, R], U8, name="dr_plane", align_bytes=64)
        bn_b = keep.tile([P, N], F32, name="bn_b")
        ident = keep.tile([P, P], F32, name="ident")

        x_rows = xf.rearrange("(p i) t -> p i t", i=PACK)
        nc.sync.dma_start(g_tab[0][:], gt[0:P, :])
        nc.sync.dma_start(list2[:], offs2)
        nc.sync.dma_start(g_tab[1][:], gt[P : 2 * P, :])
        nc.sync.dma_start(x_tab[0][:], x_rows[:, 0, :])
        nc.sync.dma_start(lists[:], offs)
        nc.sync.dma_start(cb_c[:], cb.rearrange("(q s) o -> q (s o)", s=PACK))
        nc.sync.dma_start(ra_c[:], ra.rearrange("o (q s) -> (o q) s", s=PACK))
        nc.sync.dma_start(fk_c[:], fkr.rearrange("o (p i) -> (o p) i", i=PACK))
        for i in range(1, PACK):
            nc.sync.dma_start(x_tab[i][:], x_rows[:, i, :])
        warm = keep.tile([P, 2], F32, name="warm")
        nc.vector.memset(warm[:, 0:1], 1.0)
        nc.scalar.activation(warm[:, 1:2], warm[:, 0:1], ACT.Abs_reciprocal_sqrt)
        nc.gpsimd.memset(dr_plane[:].bitcast(I32), 0)
        make_identity(nc, ident[:])
        nc.sync.dma_start(
            dr_codes[:].bitcast(I32),
            dr_words[0].rearrange("p c r -> p (c r)").bitcast(I32),
        )
        for q in range(4):
            nc.sync.dma_start(
                dr_plane[32 * q : 32 * q + 4, :].bitcast(I32),
                dr_scales[0, 4 * q : 4 * q + 4, :].bitcast(I32),
            )
        nc.sync.dma_start(bn_b[:], bn[0].partition_broadcast(P))

        half = J // 2
        hc = half // 16

        def gather_split(dst, table, offsets):
            nc.vector.tensor_copy(dst[:, 0:half], table[:].indirect(offsets[:, 0:hc]))
            nc.scalar.activation(dst[:, half:J], table[:].indirect(offsets[:, hc : 2 * hc]), ACT.Copy)

        g_abs = [keep.tile([P, PACK, P + 4 * m], F32, name="g_abs%d" % m, tag="g_abs%d" % m) for m in range(2)]
        g_bank = []
        for m in range(2):
            picked = keep.tile([P, J], F32, name="g_picked%d" % m, tag="g_picked0" if m == 0 else "ring1")
            gather_split(picked, g_tab[m], list2)
            bank = psum.tile([P, PACK, P], F32, name="g_bank%d" % m, tag="gv%d" % m)
            for s in range(PACK):
                nc.tensor.transpose(bank[:, s, :], picked[:, s:J:PACK], ident[:])
            g_bank.append(bank)

        ra_bank = psum.tile([P, PACK, P], F32, name="ra_bank")
        for s in range(PACK):
            nc.tensor.transpose(ra_bank[:, s, :], ra_c[:, s : s + 1].to_broadcast([P, P]), ident[:])

        cb_inv = keep.tile([P, PACK], F32, name="cb_inv")
        nc.vector.reciprocal(cb_inv[:], cb_c[:])
        x_picked = {}
        u_grouped = {
            first: keep.tile([P, count * J], BF16, name="u_grouped%d" % first, align_bytes=64)
            for first, count in ((0, 2), (2, 1), (3, 1))
        }
        u_codes = keep.tile([P, PACK * P], U32, name="u_codes", align_bytes=64)
        u_plane = keep.tile([P, PACK * P], U8, name="u_plane", align_bytes=64)
        u_early = psum.tile([P, 2, 2, P], F32, name="u_early")
        u_late = [psum.tile([P, 1, 2, P], F32, name="u_late%d" % i) for i in range(2)]
        u_bank = [u_early[:, 0], u_early[:, 1], u_late[0][:, 0], u_late[1][:, 0]]

        def weigh(i):
            rounded = keep.tile([P, J], BF16, name="u_rounded%d" % i, tag=("x_tab1", "g_abs1", "g_max", "round3")[i])
            nc.vector.scalar_tensor_tensor(
                out=rounded[:].rearrange("p (q s) -> p q s", s=PACK),
                in0=x_picked[i][:].rearrange("p (q s) -> p q s", s=PACK),
                scalar=fk_c[:, i : i + 1],
                in1=ra_bank[:].rearrange("p s q -> p q s"),
                op0=ALU.mult,
                op1=ALU.mult,
            )
            words = rounded[:].bitcast(F32)
            for u in range(2):
                nc.tensor.transpose(u_bank[i][:, u, :], words[:, u : J // 2 : 2], ident[:])

        def regroup(bank, first, count):
            nc.scalar.copy(
                u_grouped[first][:].bitcast(F32).rearrange("q (i p u) -> q i p u", i=count, u=2),
                bank[:].rearrange("q i u p -> q i p u"),
            )

        def quantise_u(first, count):
            cols = slice(first * P, (first + count) * P)
            nc.vector.quantize_mx(
                u_codes[:, cols].bitcast(E4M3),
                u_plane[:, cols],
                u_grouped[first][:],
            )

        def pick_tile(i):
            x_picked[i] = keep.tile([P, J], F32, name="x_picked%d" % i, tag="ring%d" % i)
            return x_picked[i]

        nc.scalar.activation(g_abs[0][:], g_bank[0][:], ACT.Abs)
        gather_split(pick_tile(0), x_tab[0], lists)
        nc.scalar.activation(g_abs[1][:, :, 0:P], g_bank[1][:], ACT.Abs)
        nc.vector.tensor_reduce(g_abs[1][:, :, P], g_abs[0][:], mybir.AxisListType.X, ALU.max)
        gather_split(pick_tile(1), x_tab[1], lists)
        g_max = keep.tile([P, PACK], F32, name="g_max")
        nc.vector.tensor_reduce(g_max[:], g_abs[1][:, :, 0 : P + 1], mybir.AxisListType.X, ALU.max)
        g_den = keep.tile([P, PACK], F32, name="g_den")
        nc.vector.scalar_tensor_tensor(g_den[:], g_max[:], 0.2, cb_inv[:], ALU.add, ALU.mult)
        g_fac = keep.tile([P, PACK], F32, name="g_fac")
        nc.vector.reciprocal(g_fac[:], g_den[:])
        weigh(0)
        weigh(1)
        nc.scalar.activation(pick_tile(2)[:], x_tab[2][:].indirect(lists[:]), ACT.Copy)
        weigh(2)
        nc.scalar.activation(pick_tile(3)[:], x_tab[3][:].indirect(lists[:]), ACT.Copy)
        g_grouped = keep.tile([P, N, PACK], BF16, name="g_grouped", align_bytes=64)

        def scale_g(m):
            nc.vector.tensor_tensor(
                g_grouped[:, m * P : (m + 1) * P, :],
                g_bank[m][:].rearrange("q s n -> q n s"),
                g_fac[:].unsqueeze(1).to_broadcast([P, P, PACK]),
                ALU.mult,
            )

        scale_g(0)
        weigh(3)
        scale_g(1)
        regroup(u_early, 0, 2)
        regroup(u_late[0], 2, 1)
        regroup(u_late[1], 3, 1)
        g_codes = keep.tile([P, N], U32, name="g_codes", align_bytes=64)
        g_plane = keep.tile([P, N], U8, name="g_plane", align_bytes=64)
        quantise_u(0, 2)
        for h in range(2):
            cols = slice(h * P, (h + 1) * P)
            nc.vector.quantize_mx(
                g_codes[:, cols].bitcast(E5M2),
                g_plane[:, cols],
                g_grouped[:, cols, :].rearrange("q n s -> q (n s)"),
            )
        quantise_u(2, 1)
        quantise_u(3, 1)
        w_bank = [psum.tile([P, PACK, P], F32, name="w_bank%d" % h) for h in range(2)]

        def moment(i):
            for h in range(2):
                cols = slice(h * P, (h + 1) * P)
                nc.tensor.matmul_mx(
                    out=w_bank[h][:, i, :],
                    lhsT=u_codes[:, i * P : (i + 1) * P].bitcast(E4M3),
                    lhsT_scale=u_plane[:, i * P : (i + 1) * P],
                    rhs=g_codes[:, cols].bitcast(E5M2),
                    rhs_scale=g_plane[:, cols],
                    start=True,
                    stop=True,
                )

        for i in range(PACK):
            moment(i)

        w_grouped = keep.tile([P, N, PACK], BF16, name="w_grouped", align_bytes=64)
        w_codes = keep.tile([P, N], U32, name="w_codes", align_bytes=64)
        w_plane = keep.tile([P, N], U8, name="w_plane", align_bytes=64)
        nc.vector.tensor_copy(w_grouped[:, 0:P, :], w_bank[0][:].rearrange("p i n -> p n i"))
        nc.scalar.copy(w_grouped[:, P:N, :], w_bank[1][:].rearrange("p i n -> p n i"))
        for h in range(2):
            cols = slice(h * P, (h + 1) * P)
            nc.vector.quantize_mx(
                w_codes[:, cols].bitcast(E5M2),
                w_plane[:, cols],
                w_grouped[:, cols, :].rearrange("p n i -> p (n i)"),
            )

        neg = keep.tile([P, 2, N], F32, name="neg")
        neg_sum = keep.tile([P, 2], F32, name="neg_sum")
        dev = keep.tile([P, 2, N], F32, name="dev")
        dev_abs = keep.tile([P, 2, N], F32, name="dev_abs")
        abs_sum = keep.tile([P, 2], F32, name="abs_sum")
        root = keep.tile([P, 2], F32, name="root")
        two_n = keep.tile([P, 1], F32, name="two_n")
        nc.gpsimd.memset(two_n[:], 2.0 * N)
        y = [keep.tile([P, N], F32, name="y%d" % t) for t in range(2)]
        v_bank = []
        for t in range(2):
            bank = psum.tile([P, N], F32, name="v_bank%d" % t, tag="gv%d" % t)
            v_bank.append(bank)
        for h in range(2):
            cols = slice(h * P, (h + 1) * P)
            for t in range(2):
                rows = slice(t * P, (t + 1) * P)
                nc.tensor.matmul_mx(
                    out=v_bank[t][:, cols],
                    lhsT=dr_codes[:, rows].bitcast(E4M3),
                    lhsT_scale=dr_plane[:, rows],
                    rhs=w_codes[:, cols].bitcast(E5M2),
                    rhs_scale=w_plane[:, cols],
                    start=True,
                    stop=True,
                )
        for t in range(2):
            nc.vector.scalar_tensor_tensor(
                out=neg[:, t, :],
                in0=v_bank[t][:],
                scalar=-1.0,
                in1=bn_b[:],
                op0=ALU.mult,
                op1=ALU.subtract,
                accum_out=neg_sum[:, t : t + 1],
            )
            nc.scalar.activation(
                dev_abs[:, t, :],
                neg[:, t, :],
                ACT.Abs,
                bias=neg_sum[:, t : t + 1],
                scale=-float(N),
                accum_out=abs_sum[:, t : t + 1],
            )
        for t in range(2):
            nc.vector.tensor_scalar(
                dev[:, t, :], neg[:, t, :], -float(N), neg_sum[:, t : t + 1], ALU.mult, ALU.add
            )
        for t in range(2):
            nc.scalar.activation(
                root[:, t : t + 1], abs_sum[:, t : t + 1], ACT.Abs_reciprocal_sqrt, bias=two_n[:], scale=1.0 / N
            )
        for t in range(2):
            nc.vector.tensor_scalar(
                y[t][:], dev[:, t, :], root[:, t : t + 1], root[:, t : t + 1], ALU.mult, ALU.mult
            )
        nc.sync.dma_start(out[0:P, :], y[0][:])
        nc.scalar.dma_start(out[P : 2 * P, :], y[1][:])
